import numpy as np
import ml_dtypes


def mxq(x, axis, fmt="e4m3"):
    dtype, down = {"e4m3": (ml_dtypes.float8_e4m3fn, 7), "e5m2": (ml_dtypes.float8_e5m2, 14)}[fmt]
    v = np.moveaxis(np.asarray(x, np.float32).astype(ml_dtypes.bfloat16).astype(np.float64), axis, -1)
    blocks = v.reshape(v.shape[:-1] + (-1, 32))
    amax = np.abs(blocks).max(-1, keepdims=True)
    byte = np.maximum(np.where(amax > 0, np.frexp(amax)[1] - 1 + 127, 0) - down, 1)
    scale = np.exp2(byte - 127.0)
    codes = (blocks / scale).astype(np.float32).astype(dtype).astype(np.float64)
    return np.moveaxis((codes * scale).reshape(v.shape), -1, axis)


WIDE = False


def mx_kscale(k):
    if not WIDE:
        return np.ones(k)
    levels = np.array([10, -10, 5, -5, 0])
    if k % 512:
        return np.exp2(np.random.permutation(np.resize(levels, k // 32))).repeat(32)
    a = np.empty((k // 512, 16))
    for p in range(k // 512):
        a[p, :8] = np.random.permutation(np.resize(levels, 8))
        for g in range(8):
            far = levels[np.abs(levels - a[p, g]) >= 10]
            a[p, g + 8] = far[np.random.randint(len(far))]
    return np.exp2(a.ravel()).repeat(32)


def f64(x):
    return np.asarray(x).astype(np.float64)


def striped(idx):
    return np.tile(np.asarray(idx).reshape(-1, 16).T, (8, 1)).astype(np.uint16)


def unstriped(offs):
    return offs[:16].T.reshape(-1).astype(np.int64)


E2M1 = np.array([0.0, 0.5, 1.0, 1.5, 2.0, 3.0, 4.0, 6.0, -0.0, -0.5, -1.0, -1.5, -2.0, -3.0, -4.0, -6.0])


def pack_weight(w, fmt):
    k, n = w.shape
    w = f64(np.asarray(w, np.float32).astype(ml_dtypes.bfloat16)).reshape(k // 32, 32, n)
    amax = np.abs(w).max(1)
    if fmt == "e4m3":
        byte = np.frexp(amax)[1] - 1 + 127 - 7
    else:
        mant, ex = np.frexp(amax / 6.0)
        byte = np.where(mant > 0.5, ex, ex - 1) + 127
    byte = np.clip(np.where(amax > 0, byte, 1), 1, 254)
    scaled = (w * np.exp2(127.0 - byte)[:, None, :]).reshape(k, n).astype(np.float32)
    by_word = np.ascontiguousarray(scaled.reshape(k // 512, 128, 4, n).transpose(0, 1, 3, 2))
    if fmt == "e4m3":
        words = by_word.astype(ml_dtypes.float8_e4m3fn).view(np.uint8)
    else:
        c = by_word.astype(ml_dtypes.float4_e2m1fn).view(np.uint8) & 0xF
        words = (c[..., 0::2] | (c[..., 1::2] << 4)).reshape(k // 512, 128, 2 * n)
    return np.ascontiguousarray(words), np.ascontiguousarray(byte.astype(np.uint8).reshape(k // 512, 16, n))


def unpack_weight(words, scales, fmt):
    g, _, n = scales.shape
    words = np.ascontiguousarray(words).reshape(g, 128, n, -1)
    if fmt == "e4m3":
        vals = words.view(ml_dtypes.float8_e4m3fn).astype(np.float64)
    else:
        nib = np.empty((g, 128, n, 4), np.uint8)
        nib[..., 0::2] = words & 0xF
        nib[..., 1::2] = words >> 4
        vals = E2M1[nib]
    vals = vals * np.repeat(np.exp2(scales.astype(np.float64) - 127.0), 8, axis=1)[..., None]
    return vals.transpose(0, 1, 3, 2).reshape(g * 512, n)


D, E, T, I, Q, G = 512, 512, 2048, 512, 128, 64


def setup_inputs():
    n = np.random.standard_normal
    idx = np.random.permutation(T)[:I]
    fd = mx_kscale(D)
    fi = mx_kscale(I)
    ti = np.ones(T)
    ti[idx] = fi
    keysp = pack_weight(n((D, T)) / fd[:, None], "e2m1")
    return {
        "query": (n((D, Q)) * 0.8 / np.sqrt(D) * fd[:, None]).astype(np.float32),
        "query2": (n((D, Q)) * 0.8 / np.sqrt(D) * fd[:, None]).astype(np.float32),
        "keys_words": keysp[0],
        "keys_scales": keysp[1],
        "dquery": (n((D, Q)) * 0.6 / np.sqrt(D) * fd[:, None]).astype(np.float32),
        "os": (np.random.uniform(4.0, 16.0, (1, I)) * fi).astype(np.float32),
        "vals": (n((E, T)) / ti).astype(np.float32),
        "offs": striped(idx),
    }


def reference(query, query2, keys_words, keys_scales, dquery, os, vals, offs):
    idx = unstriped(offs)
    keysu = unpack_weight(keys_words, keys_scales, "e2m1")
    queryq = mxq(f64(query), 0, "e4m3")
    keysidxg = keysu[:, idx]
    a = queryq.T @ keysidxg
    dqueryq = mxq(f64(dquery), 0, "e4m3")
    ta = dqueryq.T @ keysidxg
    query2q = mxq(f64(query2), 0, "e4m3")
    b = query2q.T @ keysidxg
    pa = np.exp(a)
    sa = pa.reshape(Q, G, I // G).sum(axis=2)
    z = np.sum(sa, axis=1, keepdims=True)
    pb = np.exp(b)
    sb = pb.reshape(Q, G, I // G).sum(axis=2)
    tpa = ta * pa
    tsa = tpa.reshape(Q, G, I // G).sum(axis=2)
    tz = np.sum(tsa, axis=1, keepdims=True)
    tr = (tsa - tz * sa / z) / z / sb
    trr = np.repeat(tr, I // G, axis=1)
    tw = trr * pb
    wo1 = tw * f64(os)
    wt1 = wo1.T
    vt1 = f64(vals)[:, idx].T
    wt1q = mxq(wt1, 0, "e4m3")
    vt1q = mxq(vt1, 0, "e4m3")
    o = wt1q.T @ vt1q
    return o

@@ -1,0 +1,247 @@
+from contextlib import ExitStack
+
+import concourse.mybir as mybir
+from concourse.masks import make_identity
+
+D, E, T, I, Q, G = 512, 512, 2048, 512, 128, 64
+FLOPS = 2 * Q * I * (3 * D + E)
+
+F32 = mybir.dt.float32
+BF16 = mybir.dt.bfloat16
+I32 = mybir.dt.int32
+U32 = mybir.dt.uint32
+U16 = mybir.dt.uint16
+U8 = mybir.dt.uint8
+FP8X4 = mybir.dt.float8_e4m3fn_x4
+FP4X4 = mybir.dt.float4_e2m1fn_x4
+ALU = mybir.AluOpType
+ACT = mybir.ActivationFunctionType
+AX = mybir.AxisListType
+
+P = 128
+PACK = 4
+PAGE = I // G
+E_BLOCKS = E // P
+
+
+def tile_attend_ttpagethensecond_kernel(tc, query, query2, keys_words, keys_scales, dquery, slot_factor, vals, offs, out):
+    nc = tc.nc
+    with ExitStack() as ctx:
+        keep = ctx.enter_context(tc.tile_pool(name="keep", bufs=1))
+        psum = ctx.enter_context(tc.psum_pool(name="psum", bufs=1))
+
+        offsets = keep.tile([P, I // 16], U16, name="offsets")
+        nc.sync.dma_start(offsets[:], offs)
+
+        key_scale_pool = keep.tile([P, T], U8, name="key_scale_pool")
+        nc.gpsimd.memset(key_scale_pool[:].bitcast(I32), 0)
+        for quad in range(4):
+            nc.scalar.dma_start(
+                key_scale_pool[32 * quad : 32 * quad + 4, :].bitcast(I32),
+                keys_scales[0, 4 * quad : 4 * quad + 4, :].bitcast(I32),
+            )
+        key_word_pool = keep.tile([P, T], U16, name="key_word_pool")
+        nc.sync.dma_start(key_word_pool[:].bitcast(I32), keys_words[0].bitcast(I32))
+        q_raw = {}
+        for name, src in (("a", query), ("b", query2), ("ta", dquery)):
+            q_raw[name] = keep.tile([P, PACK, Q], F32, name="q_raw_" + name)
+            nc.sync.dma_start(q_raw[name][:], src.rearrange("(p j) q -> p j q", j=PACK))
+        val_halves = []
+        for half in range(2):
+            half_tile = keep.tile([P, T // 2], F32, name="val_half_%d" % half, tag="val_half_%d" % half)
+            nc.sync.dma_start(half_tile[:], vals[0:P, half * T // 2 : (half + 1) * T // 2])
+            val_halves.append(half_tile)
+        os_col = keep.tile([P, PACK], F32, name="os_col")
+        nc.sync.dma_start(os_col[:], slot_factor[0].rearrange("(p t) -> p t", t=PACK))
+        val_pool = {}
+        for blk in range(1, E_BLOCKS):
+            val_pool[blk] = keep.tile([P, T], F32, name="val_pool_%d" % blk, tag="val_pool_%d" % blk, align_bytes=64)
+            nc.sync.dma_start(val_pool[blk][:], vals[blk * P : (blk + 1) * P, :])
+
+        ident = keep.tile([P, P], F32, name="ident")
+        make_identity(nc, ident[:])
+
+        q_codes, q_scales = {}, {}
+
+        def interleave_query(name, on_vector):
+            grouped = keep.tile([P, Q * PACK], BF16, name="q_grouped_" + name, align_bytes=64)
+            dst = grouped[:].rearrange("p (c i t) -> p c t i", i=4, t=PACK)
+            src = q_raw[name][:].rearrange("p t (c i) -> p c t i", i=4)
+            if on_vector:
+                nc.vector.tensor_copy(dst, src)
+            else:
+                nc.scalar.activation(dst, src, ACT.Copy)
+            return grouped
+
+        def quantize_query(name, grouped):
+            q_codes[name] = keep.tile([P, Q], U32, name="q_codes_" + name, align_bytes=64)
+            q_scales[name] = keep.tile([P, Q], U8, name="q_scales_" + name, align_bytes=64)
+            nc.vector.quantize_mx(out=q_codes[name][:].bitcast(FP8X4), scales=q_scales[name][:], in_=grouped[:])
+
+        key_scales = keep.tile([P, I], U8, name="key_scales", align_bytes=64)
+        nc.vector.tensor_copy(key_scales[:], key_scale_pool[:].indirect(offsets[:]))
+        key_words = keep.tile([P, I], U16, name="key_words", align_bytes=64)
+        nc.vector.tensor_copy(key_words[:], key_word_pool[:].indirect(offsets[:]))
+        for name in ("a", "b", "ta"):
+            quantize_query(name, interleave_query(name, False))
+
+        score = {}
+        for name in ("a", "b", "ta"):
+            score[name] = psum.tile([P, I], F32, name="score_" + name, tag="score", bufs=3)
+            nc.tensor.matmul_mx(
+                out=score[name][:],
+                lhsT=q_codes[name][:].bitcast(FP8X4),
+                lhsT_scale=q_scales[name][:],
+                rhs=key_words[:].bitcast(FP4X4),
+                rhs_scale=key_scales[:],
+                start=True,
+                stop=True,
+            )
+
+        neg_max_a = keep.tile([P, 1], F32, name="neg_max_a")
+        nc.vector.tensor_reduce(neg_max_a[:], score["a"][:], AX.X, ALU.max, negate=True)
+        page_max_b = keep.tile([P, G], F32, name="page_max_b")
+        nc.vector.tensor_reduce(page_max_b[:], score["b"][:].rearrange("p (g j) -> p g j", j=PAGE), AX.X, ALU.max)
+
+        val_bf16 = keep.tile([P, T], BF16, name="val_bf16")
+        nc.scalar.activation(val_bf16[:, 0 : T // 2], val_halves[0][:], ACT.Copy)
+        pa_tpa = keep.tile([P, PAGE, 2 * G], F32, name="pa_tpa", tag="val_half_0")
+        z = keep.tile([P, 1], F32, name="z")
+        nc.scalar.activation(
+            pa_tpa[:, :, 0:G],
+            score["a"][:].rearrange("p (g j) -> p j g", j=PAGE),
+            ACT.Exp,
+            bias=neg_max_a[:],
+            accum_out=z[:],
+        )
+        b_shifted = keep.tile([P, PACK, P], F32, name="b_shifted")
+        nc.vector.tensor_tensor(
+            b_shifted[:].rearrange("p t (g h) -> p t g h", h=2),
+            score["b"][:].rearrange("p (g h t) -> p t g h", h=2, t=PACK),
+            page_max_b[:].unsqueeze(1).unsqueeze(3).broadcast_to([P, PACK, G, 2]),
+            ALU.subtract,
+        )
+        tz = keep.tile([P, 1], F32, name="tz")
+        nc.vector.scalar_tensor_tensor(
+            pa_tpa[:, :, G : 2 * G],
+            score["ta"][:].rearrange("p (g j) -> p j g", j=PAGE),
+            1.0,
+            pa_tpa[:, :, 0:G],
+            ALU.mult,
+            ALU.mult,
+            accum_out=tz[:],
+        )
+        pb = keep.tile([P, PACK, P], F32, name="pb")
+        nc.scalar.activation(pb[:], b_shifted[:], ACT.Exp)
+
+        nc.scalar.activation(val_bf16[:, T // 2 : T], val_halves[1][:], ACT.Copy)
+
+        sums_a_t = psum.tile([P, Q], F32, name="sums_a_t")
+        for j in range(PAGE):
+            nc.tensor.matmul(sums_a_t[:], pa_tpa[:, j, :], ident[:], start=(j == 0), stop=(j == PAGE - 1), is_transpose=True)
+        pb_t = psum.tile([P, PACK, Q], F32, name="pb_t")
+        for t in range(PACK):
+            nc.tensor.transpose(pb_t[:, t, :], pb[:, t, :], ident[:])
+
+        sums_a_sb = keep.tile([P, Q], F32, name="sums_a_sb", tag="sums_a_sb")
+        nc.scalar.copy(sums_a_sb[:], sums_a_t[:])
+        sa_tsa = psum.tile([P, P], F32, name="sa_tsa", tag="score", bufs=3)
+        nc.tensor.transpose(sa_tsa[:], sums_a_sb[:], ident[:])
+
+        pbo_t = keep.tile([P, PACK, Q], F32, name="pbo_t")
+        for t in range(PACK):
+            nc.scalar.activation(pbo_t[:, t, :], pb_t[:, t, :], ACT.Copy, scale=os_col[:, t : t + 1])
+
+        rz = keep.tile([P, 1], F32, name="rz")
+        nc.vector.reciprocal(rz[:], z[:])
+        sb = keep.tile([P, G], F32, name="sb")
+        nc.vector.tensor_reduce(sb[:], pb[:].rearrange("p t (g h) -> p g t h", h=2), AX.XY, ALU.add)
+        neg_mean = keep.tile([P, 1], F32, name="neg_mean")
+        nc.vector.tensor_scalar(neg_mean[:], tz[:], rz[:], -1.0, ALU.mult, ALU.mult)
+        rsb = keep.tile([P, G], F32, name="rsb")
+        nc.vector.reciprocal(rsb[:], sb[:])
+        coef = keep.tile([P, 2, G], F32, name="coef")
+        nc.vector.tensor_scalar(coef[:, 1, :], rsb[:], rz[:], None, ALU.mult)
+        nc.vector.tensor_scalar(coef[:, 0, :], rsb[:], rz[:], neg_mean[:], ALU.mult, ALU.mult)
+
+        v_grouped = {}
+        grouped_01 = keep.tile([P, 2 * P * PACK], BF16, name="v_grouped_01", align_bytes=64)
+        v_grouped[0] = grouped_01[:, 0 : P * PACK]
+        v_grouped[1] = grouped_01[:, P * PACK : 2 * P * PACK]
+        for blk in (2, 3):
+            v_grouped[blk] = keep.tile([P, P * PACK], BF16, name="v_grouped_%d" % blk, align_bytes=64)[:]
+
+        def turn_values(blk, picked):
+            pairs = picked[:].bitcast(F32)
+            turned = psum.tile([P, 2, P], F32, name="v_turned", tag="v_turned", bufs=2)
+            for u in range(2):
+                nc.tensor.transpose(turned[:, u, :], pairs[:, u : I // 2 : 2], ident[:])
+            nc.scalar.copy(
+                v_grouped[blk].bitcast(F32).rearrange("p (e u) -> p e u", u=2),
+                turned[:].rearrange("p u e -> p e u"),
+            )
+
+        def pick_on_vector(blk):
+            picked = keep.tile([P, I], BF16, name="v_picked_%d" % blk)
+            nc.vector.tensor_copy(picked[:], val_pool[blk][:].indirect(offsets[:]))
+            turn_values(blk, picked)
+
+        pick_on_vector(1)
+
+        terms = keep.tile([P, 2, P], F32, name="terms")
+        nc.vector.tensor_tensor(
+            terms[:].rearrange("p w (g h) -> p w g h", h=2),
+            sa_tsa[:].rearrange("p (w g) -> p w g", w=2).unsqueeze(3).broadcast_to([P, 2, G, 2]),
+            coef[:].unsqueeze(3).broadcast_to([P, 2, G, 2]),
+            ALU.mult,
+        )
+        tr_t = psum.tile([P, Q], F32, name="tr_t", tag="score", bufs=3)
+        for w in range(2):
+            nc.tensor.matmul(tr_t[:], terms[:, w, :], ident[:], start=(w == 0), stop=(w == 1), is_transpose=True)
+
+        picked_0 = keep.tile([P, I], BF16, name="v_picked_0", tag="sums_a_sb")
+        nc.scalar.activation(picked_0[:], val_bf16[:].indirect(offsets[:]), ACT.Copy)
+        turn_values(0, picked_0)
+
+        pick_on_vector(2)
+
+        w_grouped = keep.tile([P, Q * PACK], BF16, name="w_grouped", tag="val_pool_2", align_bytes=64)
+        nc.vector.tensor_tensor(
+            w_grouped[:].rearrange("p (c i t) -> p c t i", i=4, t=PACK),
+            tr_t[:].rearrange("p (c i) -> p c i", i=4).unsqueeze(2).broadcast_to([P, Q // 4, PACK, 4]),
+            pbo_t[:].rearrange("p t (c i) -> p c t i", i=4),
+            ALU.mult,
+        )
+
+        pick_on_vector(3)
+
+        codes = keep.tile([P, Q + E], U32, name="codes", tag="val_pool_3", align_bytes=64)
+        w_codes, v_codes = codes[:, 0:Q], codes[:, Q : Q + E]
+        w_scales = keep.tile([P, Q], U8, name="w_scales", align_bytes=64)
+        v_scales = keep.tile([P, E], U8, name="v_scales", align_bytes=64)
+        nc.vector.quantize_mx(out=w_codes.bitcast(FP8X4), scales=w_scales[:], in_=w_grouped[:])
+        for a, b, src in ((0, 2 * P, grouped_01[:]), (2 * P, 3 * P, v_grouped[2]), (3 * P, E, v_grouped[3])):
+            nc.vector.quantize_mx(out=v_codes[:, a:b].bitcast(FP8X4), scales=v_scales[:, a:b], in_=src)
+
+        for lo, hi, pieces in ((0, 3 * P, ((0, 2 * P), (2 * P, 3 * P))), (3 * P, E, ((3 * P, E),))):
+            if lo == 0:
+                acc = psum.tile([Q, hi - lo], F32, name="acc_first")
+            else:
+                acc = psum.tile([Q, hi - lo], F32, name="acc_last", tag="score", bufs=3)
+            for a, b in pieces:
+                nc.tensor.matmul_mx(
+                    out=acc[:, a - lo : b - lo],
+                    lhsT=w_codes.bitcast(FP8X4),
+                    lhsT_scale=w_scales[:],
+                    rhs=v_codes[:, a:b].bitcast(FP8X4),
+                    rhs_scale=v_scales[:, a:b],
+                    start=True,
+                    stop=True,
+                )
+            result = keep.tile([Q, hi - lo], F32, name="result_%d" % lo)
+            if lo == 0:
+                nc.scalar.copy(result[:], acc[:])
+                nc.scalar.dma_start(out[:, lo:hi], result[:])
+            else:
+                nc.vector.tensor_copy(result[:], acc[:])
+                nc.sync.dma_start(out[:, lo:hi], result[:])

@@ -28,6 +28,7 @@ def tile_attend_ttpagethensecond_kernel(tc, query, query2, keys_words, keys_scal
     nc = tc.nc
     with ExitStack() as ctx:
         keep = ctx.enter_context(tc.tile_pool(name="keep", bufs=1))
+        tail = ctx.enter_context(tc.tile_pool(name="tail", bufs=1))
         psum = ctx.enter_context(tc.psum_pool(name="psum", bufs=1))
 
         offsets = keep.tile([P, I // 16], U16, name="offsets")
@@ -44,7 +45,7 @@ def tile_attend_ttpagethensecond_kernel(tc, query, query2, keys_words, keys_scal
         nc.sync.dma_start(key_word_pool[:].bitcast(I32), keys_words[0].bitcast(I32))
         q_raw = {}
         for name, src in (("a", query), ("b", query2), ("ta", dquery)):
-            q_raw[name] = keep.tile([P, PACK, Q], F32, name="q_raw_" + name)
+            q_raw[name] = keep.tile([P, PACK, Q], F32, name="q_raw_" + name, tag="q_raw_" + name, align_bytes=64)
             nc.sync.dma_start(q_raw[name][:], src.rearrange("(p j) q -> p j q", j=PACK))
         val_halves = []
         for half in range(2):
@@ -55,8 +56,12 @@ def tile_attend_ttpagethensecond_kernel(tc, query, query2, keys_words, keys_scal
         nc.sync.dma_start(os_col[:], slot_factor[0].rearrange("(p t) -> p t", t=PACK))
         val_pool = {}
         for blk in range(1, E_BLOCKS):
-            val_pool[blk] = keep.tile([P, T], F32, name="val_pool_%d" % blk, tag="val_pool_%d" % blk, align_bytes=64)
+            if blk == E_BLOCKS - 1:
+                val_pool[blk] = tail.tile([P, T], F32, name="val_pool_last", align_bytes=64, offset=0)
+            else:
+                val_pool[blk] = keep.tile([P, T], F32, name="val_pool_%d" % blk)
             nc.sync.dma_start(val_pool[blk][:], vals[blk * P : (blk + 1) * P, :])
+
 
         ident = keep.tile([P, P], F32, name="ident")
         make_identity(nc, ident[:])
@@ -78,91 +83,88 @@ def tile_attend_ttpagethensecond_kernel(tc, query, query2, keys_words, keys_scal
             q_scales[name] = keep.tile([P, Q], U8, name="q_scales_" + name, align_bytes=64)
             nc.vector.quantize_mx(out=q_codes[name][:].bitcast(FP8X4), scales=q_scales[name][:], in_=grouped[:])
 
-        key_scales = keep.tile([P, I], U8, name="key_scales", align_bytes=64)
-        nc.vector.tensor_copy(key_scales[:], key_scale_pool[:].indirect(offsets[:]))
         key_words = keep.tile([P, I], U16, name="key_words", align_bytes=64)
         nc.vector.tensor_copy(key_words[:], key_word_pool[:].indirect(offsets[:]))
-        for name in ("a", "b", "ta"):
+        quantize_query("a", interleave_query("a", False))
+        key_scales = keep.tile([P, I], U8, name="key_scales", tag="q_raw_a", align_bytes=64)
+        for half in range(2):
+            nc.vector.tensor_copy(
+                key_scales[:, half * I // 2 : (half + 1) * I // 2],
+                key_scale_pool[:].indirect(offsets[:, half * I // 32 : (half + 1) * I // 32]),
+            )
+        for name in ("b", "ta"):
             quantize_query(name, interleave_query(name, False))
 
         score = {}
-        for name in ("a", "b", "ta"):
-            score[name] = psum.tile([P, I], F32, name="score_" + name, tag="score", bufs=3)
-            nc.tensor.matmul_mx(
-                out=score[name][:],
-                lhsT=q_codes[name][:].bitcast(FP8X4),
-                lhsT_scale=q_scales[name][:],
-                rhs=key_words[:].bitcast(FP4X4),
-                rhs_scale=key_scales[:],
-                start=True,
-                stop=True,
-            )
+        for name, width in (("a", I // 2), ("b", I), ("ta", I)):
+            score[name] = psum.tile([P, I], F32, name="score_" + name, tag="bank_" + name)
+            for lo in range(0, I, width):
+                nc.tensor.matmul_mx(
+                    out=score[name][:, lo : lo + width],
+                    lhsT=q_codes[name][:].bitcast(FP8X4),
+                    lhsT_scale=q_scales[name][:],
+                    rhs=key_words[:, lo : lo + width].bitcast(FP4X4),
+                    rhs_scale=key_scales[:, lo : lo + width],
+                    start=True,
+                    stop=True,
+                )
 
         neg_max_a = keep.tile([P, 1], F32, name="neg_max_a")
         nc.vector.tensor_reduce(neg_max_a[:], score["a"][:], AX.X, ALU.max, negate=True)
         page_max_b = keep.tile([P, G], F32, name="page_max_b")
         nc.vector.tensor_reduce(page_max_b[:], score["b"][:].rearrange("p (g j) -> p g j", j=PAGE), AX.X, ALU.max)
 
-        val_bf16 = keep.tile([P, T], BF16, name="val_bf16")
+        val_bf16 = keep.tile([P, T], BF16, name="val_bf16", tag="val_bf16")
         nc.scalar.activation(val_bf16[:, 0 : T // 2], val_halves[0][:], ACT.Copy)
-        pa_tpa = keep.tile([P, PAGE, 2 * G], F32, name="pa_tpa", tag="val_half_0")
+        pa_tpa = keep.tile([P, 2 * I], F32, name="pa_tpa", tag="val_half_0")
+        pa, tpa = pa_tpa[:, 0:I], pa_tpa[:, I : 2 * I]
         z = keep.tile([P, 1], F32, name="z")
-        nc.scalar.activation(
-            pa_tpa[:, :, 0:G],
-            score["a"][:].rearrange("p (g j) -> p j g", j=PAGE),
-            ACT.Exp,
-            bias=neg_max_a[:],
-            accum_out=z[:],
-        )
-        b_shifted = keep.tile([P, PACK, P], F32, name="b_shifted")
+        nc.scalar.activation(pa, score["a"][:], ACT.Exp, bias=neg_max_a[:], accum_out=z[:])
+        b_shifted = keep.tile([P, I], F32, name="b_shifted")
         nc.vector.tensor_tensor(
-            b_shifted[:].rearrange("p t (g h) -> p t g h", h=2),
-            score["b"][:].rearrange("p (g h t) -> p t g h", h=2, t=PACK),
-            page_max_b[:].unsqueeze(1).unsqueeze(3).broadcast_to([P, PACK, G, 2]),
+            b_shifted[:].rearrange("p (g j) -> p g j", j=PAGE),
+            score["b"][:].rearrange("p (g j) -> p g j", j=PAGE),
+            page_max_b[:].unsqueeze(2).broadcast_to([P, G, PAGE]),
             ALU.subtract,
         )
         tz = keep.tile([P, 1], F32, name="tz")
-        nc.vector.scalar_tensor_tensor(
-            pa_tpa[:, :, G : 2 * G],
-            score["ta"][:].rearrange("p (g j) -> p j g", j=PAGE),
-            1.0,
-            pa_tpa[:, :, 0:G],
-            ALU.mult,
-            ALU.mult,
-            accum_out=tz[:],
-        )
-        pb = keep.tile([P, PACK, P], F32, name="pb")
-        nc.scalar.activation(pb[:], b_shifted[:], ACT.Exp)
-
+        nc.vector.scalar_tensor_tensor(tpa, score["ta"][:], 1.0, pa, ALU.mult, ALU.mult, accum_out=tz[:])
         nc.scalar.activation(val_bf16[:, T // 2 : T], val_halves[1][:], ACT.Copy)
+        pb = keep.tile([P, PACK, P], F32, name="pb", tag="val_half_1")
+        nc.scalar.activation(
+            pb[:].rearrange("p t s -> p s t"), b_shifted[:].rearrange("p (s t) -> p s t", t=PACK), ACT.Exp
+        )
 
-        sums_a_t = psum.tile([P, Q], F32, name="sums_a_t")
+        picked_0 = keep.tile([P, I], BF16, name="v_picked_0")
+        nc.scalar.activation(picked_0[:], val_bf16[:].indirect(offsets[:]), ACT.Copy)
+
+        rz = keep.tile([P, 1], F32, name="rz")
+        nc.vector.reciprocal(rz[:], z[:])
+        neg_mean = keep.tile([P, 1], F32, name="neg_mean")
+        nc.gpsimd.tensor_scalar(neg_mean[:], tz[:], rz[:], -1.0, ALU.mult, ALU.mult)
+        neg_mean_rz = keep.tile([P, 1], F32, name="neg_mean_rz", tag="neg_mean_rz")
+        nc.gpsimd.tensor_scalar(neg_mean_rz[:], neg_mean[:], rz[:], 1.0, ALU.mult, ALU.mult)
+
+        sums_a_t = psum.tile([P, Q], F32, name="sums_a_t", tag="bank_sums")
         for j in range(PAGE):
-            nc.tensor.matmul(sums_a_t[:], pa_tpa[:, j, :], ident[:], start=(j == 0), stop=(j == PAGE - 1), is_transpose=True)
+            nc.tensor.matmul(sums_a_t[:], pa_tpa[:, j : 2 * I : PAGE], ident[:], start=(j == 0), stop=(j == PAGE - 1), is_transpose=True)
         pb_t = psum.tile([P, PACK, Q], F32, name="pb_t")
         for t in range(PACK):
             nc.tensor.transpose(pb_t[:, t, :], pb[:, t, :], ident[:])
 
-        sums_a_sb = keep.tile([P, Q], F32, name="sums_a_sb", tag="sums_a_sb")
+        sums_a_sb = keep.tile([P, Q], F32, name="sums_a_sb", tag="val_bf16")
         nc.scalar.copy(sums_a_sb[:], sums_a_t[:])
-        sa_tsa = psum.tile([P, P], F32, name="sa_tsa", tag="score", bufs=3)
+        sa_tsa = psum.tile([P, P], F32, name="sa_tsa", tag="bank_a")
         nc.tensor.transpose(sa_tsa[:], sums_a_sb[:], ident[:])
+        parts = keep.tile([P, 2, G], F32, name="parts")
+        nc.scalar.activation(parts[:, 0, :], sa_tsa[:, 0:G], ACT.Copy, scale=neg_mean_rz[:])
+        nc.scalar.activation(parts[:, 1, :], sa_tsa[:, G : 2 * G], ACT.Copy, scale=rz[:])
+        t_share = keep.tile([P, G], F32, name="t_share")
+        nc.gpsimd.tensor_tensor(t_share[:], parts[:, 0, :], parts[:, 1, :], ALU.add)
 
-        pbo_t = keep.tile([P, PACK, Q], F32, name="pbo_t")
+        pbo_t = keep.tile([P, PACK, Q], F32, name="pbo_t", tag="neg_mean_rz")
         for t in range(PACK):
             nc.scalar.activation(pbo_t[:, t, :], pb_t[:, t, :], ACT.Copy, scale=os_col[:, t : t + 1])
-
-        rz = keep.tile([P, 1], F32, name="rz")
-        nc.vector.reciprocal(rz[:], z[:])
-        sb = keep.tile([P, G], F32, name="sb")
-        nc.vector.tensor_reduce(sb[:], pb[:].rearrange("p t (g h) -> p g t h", h=2), AX.XY, ALU.add)
-        neg_mean = keep.tile([P, 1], F32, name="neg_mean")
-        nc.vector.tensor_scalar(neg_mean[:], tz[:], rz[:], -1.0, ALU.mult, ALU.mult)
-        rsb = keep.tile([P, G], F32, name="rsb")
-        nc.vector.reciprocal(rsb[:], sb[:])
-        coef = keep.tile([P, 2, G], F32, name="coef")
-        nc.vector.tensor_scalar(coef[:, 1, :], rsb[:], rz[:], None, ALU.mult)
-        nc.vector.tensor_scalar(coef[:, 0, :], rsb[:], rz[:], neg_mean[:], ALU.mult, ALU.mult)
 
         v_grouped = {}
         grouped_01 = keep.tile([P, 2 * P * PACK], BF16, name="v_grouped_01", align_bytes=64)
@@ -173,7 +175,7 @@ def tile_attend_ttpagethensecond_kernel(tc, query, query2, keys_words, keys_scal
 
         def turn_values(blk, picked):
             pairs = picked[:].bitcast(F32)
-            turned = psum.tile([P, 2, P], F32, name="v_turned", tag="v_turned", bufs=2)
+            turned = psum.tile([P, 2, P], F32, name="v_turned_%d" % blk, tag=("bank_a", "bank_sums", "bank_v2", "bank_v3")[blk])
             for u in range(2):
                 nc.tensor.transpose(turned[:, u, :], pairs[:, u : I // 2 : 2], ident[:])
             nc.scalar.copy(
@@ -186,26 +188,27 @@ def tile_attend_ttpagethensecond_kernel(tc, query, query2, keys_words, keys_scal
             nc.vector.tensor_copy(picked[:], val_pool[blk][:].indirect(offsets[:]))
             turn_values(blk, picked)
 
+        turn_values(0, picked_0)
         pick_on_vector(1)
 
-        terms = keep.tile([P, 2, P], F32, name="terms")
-        nc.vector.tensor_tensor(
-            terms[:].rearrange("p w (g h) -> p w g h", h=2),
-            sa_tsa[:].rearrange("p (w g) -> p w g", w=2).unsqueeze(3).broadcast_to([P, 2, G, 2]),
-            coef[:].unsqueeze(3).broadcast_to([P, 2, G, 2]),
+        sb = keep.tile([P, G], F32, name="sb")
+        nc.vector.tensor_reduce(sb[:], pb[:].rearrange("p t (g h) -> p g t h", h=2), AX.XY, ALU.add)
+        rsb = keep.tile([P, G], F32, name="rsb")
+        nc.vector.reciprocal(rsb[:], sb[:])
+        tr = keep.tile([P, P], F32, name="tr")
+        nc.gpsimd.tensor_tensor(
+            tr[:].rearrange("p (g h) -> p g h", h=2),
+            t_share[:].unsqueeze(2).broadcast_to([P, G, 2]),
+            rsb[:].unsqueeze(2).broadcast_to([P, G, 2]),
             ALU.mult,
         )
-        tr_t = psum.tile([P, Q], F32, name="tr_t", tag="score", bufs=3)
-        for w in range(2):
-            nc.tensor.matmul(tr_t[:], terms[:, w, :], ident[:], start=(w == 0), stop=(w == 1), is_transpose=True)
-
-        picked_0 = keep.tile([P, I], BF16, name="v_picked_0", tag="sums_a_sb")
-        nc.scalar.activation(picked_0[:], val_bf16[:].indirect(offsets[:]), ACT.Copy)
-        turn_values(0, picked_0)
+        tr_t = psum.tile([P, Q], F32, name="tr_t", tag="bank_b")
+        nc.tensor.transpose(tr_t[:], tr[:], ident[:])
 
         pick_on_vector(2)
+        pick_on_vector(3)
 
-        w_grouped = keep.tile([P, Q * PACK], BF16, name="w_grouped", tag="val_pool_2", align_bytes=64)
+        w_grouped = tail.tile([P, Q * PACK], BF16, name="w_grouped", align_bytes=64, offset=0)
         nc.vector.tensor_tensor(
             w_grouped[:].rearrange("p (c i t) -> p c t i", i=4, t=PACK),
             tr_t[:].rearrange("p (c i) -> p c i", i=4).unsqueeze(2).broadcast_to([P, Q // 4, PACK, 4]),
@@ -213,35 +216,36 @@ def tile_attend_ttpagethensecond_kernel(tc, query, query2, keys_words, keys_scal
             ALU.mult,
         )
 
-        pick_on_vector(3)
-
-        codes = keep.tile([P, Q + E], U32, name="codes", tag="val_pool_3", align_bytes=64)
-        w_codes, v_codes = codes[:, 0:Q], codes[:, Q : Q + E]
-        w_scales = keep.tile([P, Q], U8, name="w_scales", align_bytes=64)
+        v_codes = tail.tile([P, E], U32, name="v_codes", align_bytes=64, offset=1024)
         v_scales = keep.tile([P, E], U8, name="v_scales", align_bytes=64)
-        nc.vector.quantize_mx(out=w_codes.bitcast(FP8X4), scales=w_scales[:], in_=w_grouped[:])
-        for a, b, src in ((0, 2 * P, grouped_01[:]), (2 * P, 3 * P, v_grouped[2]), (3 * P, E, v_grouped[3])):
+        w_codes = keep.tile([P, Q], U32, name="w_codes", align_bytes=64)
+        w_scales = keep.tile([P, Q], U8, name="w_scales", align_bytes=64)
+
+        def quantize_values(a, b, src):
             nc.vector.quantize_mx(out=v_codes[:, a:b].bitcast(FP8X4), scales=v_scales[:, a:b], in_=src)
 
-        for lo, hi, pieces in ((0, 3 * P, ((0, 2 * P), (2 * P, 3 * P))), (3 * P, E, ((3 * P, E),))):
-            if lo == 0:
-                acc = psum.tile([Q, hi - lo], F32, name="acc_first")
-            else:
-                acc = psum.tile([Q, hi - lo], F32, name="acc_last", tag="score", bufs=3)
-            for a, b in pieces:
-                nc.tensor.matmul_mx(
-                    out=acc[:, a - lo : b - lo],
-                    lhsT=w_codes.bitcast(FP8X4),
-                    lhsT_scale=w_scales[:],
-                    rhs=v_codes[:, a:b].bitcast(FP8X4),
-                    rhs_scale=v_scales[:, a:b],
-                    start=True,
-                    stop=True,
-                )
+        quantize_values(0, 2 * P, grouped_01[:])
+        nc.vector.quantize_mx(out=w_codes[:].bitcast(FP8X4), scales=w_scales[:], in_=w_grouped[:])
+        quantize_values(2 * P, 3 * P, v_grouped[2])
+        quantize_values(3 * P, E, v_grouped[3])
+
+        for lo, hi, bank in ((0, 2 * P, "bank_ta"), (2 * P, 3 * P, "bank_spare"), (3 * P, E, "bank_b")):
+            acc = psum.tile([Q, hi - lo], F32, name="acc_%d" % lo, tag=bank)
+            nc.tensor.matmul_mx(
+                out=acc[:],
+                lhsT=w_codes[:].bitcast(FP8X4),
+                lhsT_scale=w_scales[:],
+                rhs=v_codes[:, lo:hi].bitcast(FP8X4),
+                rhs_scale=v_scales[:, lo:hi],
+                start=True,
+                stop=True,
+            )
             result = keep.tile([Q, hi - lo], F32, name="result_%d" % lo)
-            if lo == 0:
+            if hi < E:
                 nc.scalar.copy(result[:], acc[:])
-                nc.scalar.dma_start(out[:, lo:hi], result[:])
             else:
                 nc.vector.tensor_copy(result[:], acc[:])
+            if lo == 2 * P:
+                nc.scalar.dma_start(out[:, lo:hi], result[:])
+            else:
                 nc.sync.dma_start(out[:, lo:hi], result[:])

@@ -21,7 +21,11 @@ AX = mybir.AxisListType
 P = 128
 PACK = 4
 PAGE = I // G
+QUAD = 32
+GROUP = 16
+LINE = 4
 E_BLOCKS = E // P
+MX_ALIGN = 64
 
 
 def tile_attend_ttpagethensecond_kernel(tc, query, query2, keys_words, keys_scales, dquery, slot_factor, vals, offs, out):
@@ -31,22 +35,22 @@ def tile_attend_ttpagethensecond_kernel(tc, query, query2, keys_words, keys_scal
         tail = ctx.enter_context(tc.tile_pool(name="tail", bufs=1))
         psum = ctx.enter_context(tc.psum_pool(name="psum", bufs=1))
 
-        offsets = keep.tile([P, I // 16], U16, name="offsets")
+        offsets = keep.tile([P, I // GROUP], U16, name="offsets")
         nc.sync.dma_start(offsets[:], offs)
 
         key_scale_pool = keep.tile([P, T], U8, name="key_scale_pool")
         nc.gpsimd.memset(key_scale_pool[:].bitcast(I32), 0)
-        for quad in range(4):
+        for quad in range(P // QUAD):
             nc.scalar.dma_start(
-                key_scale_pool[32 * quad : 32 * quad + 4, :].bitcast(I32),
+                key_scale_pool[QUAD * quad : QUAD * quad + 4, :].bitcast(I32),
                 keys_scales[0, 4 * quad : 4 * quad + 4, :].bitcast(I32),
             )
         key_word_pool = keep.tile([P, T], U16, name="key_word_pool")
         nc.sync.dma_start(key_word_pool[:].bitcast(I32), keys_words[0].bitcast(I32))
         q_raw = {}
         for name, src in (("a", query), ("b", query2), ("ta", dquery)):
-            q_raw[name] = keep.tile([P, PACK, Q], F32, name="q_raw_" + name, tag="q_raw_" + name, align_bytes=64)
-            nc.sync.dma_start(q_raw[name][:], src.rearrange("(p j) q -> p j q", j=PACK))
+            q_raw[name] = keep.tile([P, PACK, Q], F32, name="q_raw_" + name, tag="q_raw_" + name, align_bytes=MX_ALIGN)
+            nc.sync.dma_start(q_raw[name][:], src.rearrange("(p t) q -> p t q", t=PACK))
         val_halves = []
         for half in range(2):
             half_tile = keep.tile([P, T // 2], F32, name="val_half_%d" % half, tag="val_half_%d" % half)
@@ -57,43 +61,39 @@ def tile_attend_ttpagethensecond_kernel(tc, query, query2, keys_words, keys_scal
         val_pool = {}
         for blk in range(1, E_BLOCKS):
             if blk == E_BLOCKS - 1:
-                val_pool[blk] = tail.tile([P, T], F32, name="val_pool_last", align_bytes=64, offset=0)
+                val_pool[blk] = tail.tile([P, T], F32, name="val_pool_last", align_bytes=MX_ALIGN, offset=0)
             else:
                 val_pool[blk] = keep.tile([P, T], F32, name="val_pool_%d" % blk)
             nc.sync.dma_start(val_pool[blk][:], vals[blk * P : (blk + 1) * P, :])
-
 
         ident = keep.tile([P, P], F32, name="ident")
         make_identity(nc, ident[:])
 
         q_codes, q_scales = {}, {}
 
-        def interleave_query(name, on_vector):
-            grouped = keep.tile([P, Q * PACK], BF16, name="q_grouped_" + name, align_bytes=64)
-            dst = grouped[:].rearrange("p (c i t) -> p c t i", i=4, t=PACK)
-            src = q_raw[name][:].rearrange("p t (c i) -> p c t i", i=4)
-            if on_vector:
-                nc.vector.tensor_copy(dst, src)
-            else:
-                nc.scalar.activation(dst, src, ACT.Copy)
-            return grouped
-
-        def quantize_query(name, grouped):
-            q_codes[name] = keep.tile([P, Q], U32, name="q_codes_" + name, align_bytes=64)
-            q_scales[name] = keep.tile([P, Q], U8, name="q_scales_" + name, align_bytes=64)
+        def quantize_query(name):
+            grouped = keep.tile([P, Q * PACK], BF16, name="q_grouped_" + name, align_bytes=MX_ALIGN)
+            nc.scalar.activation(
+                grouped[:].rearrange("p (c i t) -> p c t i", i=LINE, t=PACK),
+                q_raw[name][:].rearrange("p t (c i) -> p c t i", i=LINE),
+                ACT.Copy,
+            )
+            q_codes[name] = keep.tile([P, Q], U32, name="q_codes_" + name, align_bytes=MX_ALIGN)
+            q_scales[name] = keep.tile([P, Q], U8, name="q_scales_" + name, align_bytes=MX_ALIGN)
             nc.vector.quantize_mx(out=q_codes[name][:].bitcast(FP8X4), scales=q_scales[name][:], in_=grouped[:])
 
-        key_words = keep.tile([P, I], U16, name="key_words", align_bytes=64)
+        key_words = keep.tile([P, I], U16, name="key_words", align_bytes=MX_ALIGN)
         nc.vector.tensor_copy(key_words[:], key_word_pool[:].indirect(offsets[:]))
-        quantize_query("a", interleave_query("a", False))
-        key_scales = keep.tile([P, I], U8, name="key_scales", tag="q_raw_a", align_bytes=64)
+        quantize_query("a")
+        key_scales = keep.tile([P, I], U8, name="key_scales", tag="q_raw_a", align_bytes=MX_ALIGN)
+        half_cols = I // GROUP // 2
         for half in range(2):
             nc.vector.tensor_copy(
                 key_scales[:, half * I // 2 : (half + 1) * I // 2],
-                key_scale_pool[:].indirect(offsets[:, half * I // 32 : (half + 1) * I // 32]),
+                key_scale_pool[:].indirect(offsets[:, half * half_cols : (half + 1) * half_cols]),
             )
-        for name in ("b", "ta"):
-            quantize_query(name, interleave_query(name, False))
+        quantize_query("b")
+        quantize_query("ta")
 
         score = {}
         for name, width in (("a", I // 2), ("b", I), ("ta", I)):
@@ -134,7 +134,6 @@ def tile_attend_ttpagethensecond_kernel(tc, query, query2, keys_words, keys_scal
         nc.scalar.activation(
             pb[:].rearrange("p t s -> p s t"), b_shifted[:].rearrange("p (s t) -> p s t", t=PACK), ACT.Exp
         )
-
         picked_0 = keep.tile([P, I], BF16, name="v_picked_0")
         nc.scalar.activation(picked_0[:], val_bf16[:].indirect(offsets[:]), ACT.Copy)
 
@@ -142,54 +141,52 @@ def tile_attend_ttpagethensecond_kernel(tc, query, query2, keys_words, keys_scal
         nc.vector.reciprocal(rz[:], z[:])
         neg_mean = keep.tile([P, 1], F32, name="neg_mean")
         nc.gpsimd.tensor_scalar(neg_mean[:], tz[:], rz[:], -1.0, ALU.mult, ALU.mult)
-        neg_mean_rz = keep.tile([P, 1], F32, name="neg_mean_rz", tag="neg_mean_rz")
+        neg_mean_rz = keep.tile([P, 1], F32, name="neg_mean_rz")
         nc.gpsimd.tensor_scalar(neg_mean_rz[:], neg_mean[:], rz[:], 1.0, ALU.mult, ALU.mult)
 
-        sums_a_t = psum.tile([P, Q], F32, name="sums_a_t", tag="bank_sums")
+        sums_t = psum.tile([P, Q], F32, name="sums_t")
         for j in range(PAGE):
-            nc.tensor.matmul(sums_a_t[:], pa_tpa[:, j : 2 * I : PAGE], ident[:], start=(j == 0), stop=(j == PAGE - 1), is_transpose=True)
-        pb_t = psum.tile([P, PACK, Q], F32, name="pb_t")
+            nc.tensor.matmul(
+                sums_t[:], pa_tpa[:, j : 2 * I : PAGE], ident[:], start=(j == 0), stop=(j == PAGE - 1), is_transpose=True
+            )
+        pb_t = psum.tile([P, PACK, Q], F32, name="pb_t", tag="bank_pb")
         for t in range(PACK):
             nc.tensor.transpose(pb_t[:, t, :], pb[:, t, :], ident[:])
 
-        sums_a_sb = keep.tile([P, Q], F32, name="sums_a_sb", tag="val_bf16")
-        nc.scalar.copy(sums_a_sb[:], sums_a_t[:])
-        sa_tsa = psum.tile([P, P], F32, name="sa_tsa", tag="bank_a")
-        nc.tensor.transpose(sa_tsa[:], sums_a_sb[:], ident[:])
-        parts = keep.tile([P, 2, G], F32, name="parts")
-        nc.scalar.activation(parts[:, 0, :], sa_tsa[:, 0:G], ACT.Copy, scale=neg_mean_rz[:])
-        nc.scalar.activation(parts[:, 1, :], sa_tsa[:, G : 2 * G], ACT.Copy, scale=rz[:])
+        sums_sb = keep.tile([P, Q], F32, name="sums_sb", tag="val_bf16")
+        nc.scalar.copy(sums_sb[:], sums_t[:])
+        sa_tsa = psum.tile([P, 2 * G], F32, name="sa_tsa", tag="bank_a")
+        nc.tensor.transpose(sa_tsa[:], sums_sb[:], ident[:])
+        share_parts = keep.tile([P, 2, G], F32, name="share_parts")
+        nc.scalar.activation(share_parts[:, 0, :], sa_tsa[:, 0:G], ACT.Copy, scale=neg_mean_rz[:])
+        nc.scalar.activation(share_parts[:, 1, :], sa_tsa[:, G : 2 * G], ACT.Copy, scale=rz[:])
         t_share = keep.tile([P, G], F32, name="t_share")
-        nc.gpsimd.tensor_tensor(t_share[:], parts[:, 0, :], parts[:, 1, :], ALU.add)
+        nc.gpsimd.tensor_tensor(t_share[:], share_parts[:, 0, :], share_parts[:, 1, :], ALU.add)
 
-        pbo_t = keep.tile([P, PACK, Q], F32, name="pbo_t", tag="neg_mean_rz")
+        pbo_t = keep.tile([P, PACK, Q], F32, name="pbo_t")
         for t in range(PACK):
             nc.scalar.activation(pbo_t[:, t, :], pb_t[:, t, :], ACT.Copy, scale=os_col[:, t : t + 1])
-
-        v_grouped = {}
-        grouped_01 = keep.tile([P, 2 * P * PACK], BF16, name="v_grouped_01", align_bytes=64)
-        v_grouped[0] = grouped_01[:, 0 : P * PACK]
-        v_grouped[1] = grouped_01[:, P * PACK : 2 * P * PACK]
-        for blk in (2, 3):
-            v_grouped[blk] = keep.tile([P, P * PACK], BF16, name="v_grouped_%d" % blk, align_bytes=64)[:]
-
-        def turn_values(blk, picked):
-            pairs = picked[:].bitcast(F32)
-            turned = psum.tile([P, 2, P], F32, name="v_turned_%d" % blk, tag=("bank_a", "bank_sums", "bank_v2", "bank_v3")[blk])
-            for u in range(2):
-                nc.tensor.transpose(turned[:, u, :], pairs[:, u : I // 2 : 2], ident[:])
-            nc.scalar.copy(
-                v_grouped[blk].bitcast(F32).rearrange("p (e u) -> p e u", u=2),
-                turned[:].rearrange("p u e -> p e u"),
-            )
 
         def pick_on_vector(blk):
             picked = keep.tile([P, I], BF16, name="v_picked_%d" % blk)
             nc.vector.tensor_copy(picked[:], val_pool[blk][:].indirect(offsets[:]))
-            turn_values(blk, picked)
+            return picked
 
-        turn_values(0, picked_0)
-        pick_on_vector(1)
+        def turn_values(name, picked_blocks, bank):
+            n = len(picked_blocks)
+            turned = psum.tile([P, n, 2, P], F32, name="v_turned_" + name, tag=bank)
+            for b, picked in enumerate(picked_blocks):
+                pairs = picked[:].bitcast(F32)
+                for u in range(2):
+                    nc.tensor.transpose(turned[:, b, u, :], pairs[:, u : I // 2 : 2], ident[:])
+            grouped = keep.tile([P, n * P * PACK], BF16, name="v_grouped_" + name, align_bytes=MX_ALIGN)
+            nc.scalar.copy(
+                grouped[:].bitcast(F32).rearrange("p (b e u) -> p b e u", b=n, u=2),
+                turned[:].rearrange("p b u e -> p b e u"),
+            )
+            return grouped
+
+        grouped_01 = turn_values("01", [picked_0, pick_on_vector(1)], "bank_a")
 
         sb = keep.tile([P, G], F32, name="sb")
         nc.vector.tensor_reduce(sb[:], pb[:].rearrange("p t (g h) -> p g t h", h=2), AX.XY, ALU.add)
@@ -205,31 +202,30 @@ def tile_attend_ttpagethensecond_kernel(tc, query, query2, keys_words, keys_scal
         tr_t = psum.tile([P, Q], F32, name="tr_t", tag="bank_b")
         nc.tensor.transpose(tr_t[:], tr[:], ident[:])
 
-        pick_on_vector(2)
-        pick_on_vector(3)
+        grouped_2 = turn_values("2", [pick_on_vector(2)], "bank_pb")
+        grouped_3 = turn_values("3", [pick_on_vector(3)], "bank_v3")
 
-        w_grouped = tail.tile([P, Q * PACK], BF16, name="w_grouped", align_bytes=64, offset=0)
+        w_grouped = tail.tile([P, Q * PACK], BF16, name="w_grouped", align_bytes=MX_ALIGN, offset=0)
+        v_codes = tail.tile([P, E], U32, name="v_codes", align_bytes=MX_ALIGN, offset=2 * Q * PACK)
+        v_scales = keep.tile([P, E], U8, name="v_scales", align_bytes=MX_ALIGN)
+        w_codes = keep.tile([P, Q], U32, name="w_codes", align_bytes=MX_ALIGN)
+        w_scales = keep.tile([P, Q], U8, name="w_scales", align_bytes=MX_ALIGN)
+
+        def quantize_values(lo, hi, grouped):
+            nc.vector.quantize_mx(out=v_codes[:, lo:hi].bitcast(FP8X4), scales=v_scales[:, lo:hi], in_=grouped[:])
+
         nc.vector.tensor_tensor(
-            w_grouped[:].rearrange("p (c i t) -> p c t i", i=4, t=PACK),
-            tr_t[:].rearrange("p (c i) -> p c i", i=4).unsqueeze(2).broadcast_to([P, Q // 4, PACK, 4]),
-            pbo_t[:].rearrange("p t (c i) -> p c t i", i=4),
+            w_grouped[:].rearrange("p (c i t) -> p c t i", i=LINE, t=PACK),
+            tr_t[:].rearrange("p (c i) -> p c i", i=LINE).unsqueeze(2).broadcast_to([P, Q // LINE, PACK, LINE]),
+            pbo_t[:].rearrange("p t (c i) -> p c t i", i=LINE),
             ALU.mult,
         )
-
-        v_codes = tail.tile([P, E], U32, name="v_codes", align_bytes=64, offset=1024)
-        v_scales = keep.tile([P, E], U8, name="v_scales", align_bytes=64)
-        w_codes = keep.tile([P, Q], U32, name="w_codes", align_bytes=64)
-        w_scales = keep.tile([P, Q], U8, name="w_scales", align_bytes=64)
-
-        def quantize_values(a, b, src):
-            nc.vector.quantize_mx(out=v_codes[:, a:b].bitcast(FP8X4), scales=v_scales[:, a:b], in_=src)
-
-        quantize_values(0, 2 * P, grouped_01[:])
+        quantize_values(0, 2 * P, grouped_01)
         nc.vector.quantize_mx(out=w_codes[:].bitcast(FP8X4), scales=w_scales[:], in_=w_grouped[:])
-        quantize_values(2 * P, 3 * P, v_grouped[2])
-        quantize_values(3 * P, E, v_grouped[3])
+        quantize_values(2 * P, 3 * P, grouped_2)
+        quantize_values(3 * P, E, grouped_3)
 
-        for lo, hi, bank in ((0, 2 * P, "bank_ta"), (2 * P, 3 * P, "bank_spare"), (3 * P, E, "bank_b")):
+        for lo, hi, bank in ((0, 2 * P, "bank_ta"), (2 * P, 3 * P, "bank_out"), (3 * P, E, "bank_b")):
             acc = psum.tile([Q, hi - lo], F32, name="acc_%d" % lo, tag=bank)
             nc.tensor.matmul_mx(
                 out=acc[:],

from contextlib import ExitStack

import concourse.mybir as mybir
from concourse.masks import make_identity

D, E, T, I, Q, G = 512, 512, 2048, 512, 128, 64
FLOPS = 2 * Q * I * (3 * D + E)

F32 = mybir.dt.float32
BF16 = mybir.dt.bfloat16
I32 = mybir.dt.int32
U32 = mybir.dt.uint32
U16 = mybir.dt.uint16
U8 = mybir.dt.uint8
FP8X4 = mybir.dt.float8_e4m3fn_x4
FP4X4 = mybir.dt.float4_e2m1fn_x4
ALU = mybir.AluOpType
ACT = mybir.ActivationFunctionType
AX = mybir.AxisListType

P = 128
PACK = 4
PAGE = I // G
QUAD = 32
GROUP = 16
LINE = 4
E_BLOCKS = E // P
MX_ALIGN = 64


def tile_attend_ttpagethensecond_kernel(tc, query, query2, keys_words, keys_scales, dquery, slot_factor, vals, offs, out):
    nc = tc.nc
    with ExitStack() as ctx:
        keep = ctx.enter_context(tc.tile_pool(name="keep", bufs=1))
        tail = ctx.enter_context(tc.tile_pool(name="tail", bufs=1))
        psum = ctx.enter_context(tc.psum_pool(name="psum", bufs=1))

        offsets = keep.tile([P, I // GROUP], U16, name="offsets")
        nc.sync.dma_start(offsets[:], offs)

        key_scale_pool = keep.tile([P, T], U8, name="key_scale_pool")
        nc.gpsimd.memset(key_scale_pool[:].bitcast(I32), 0)
        for quad in range(P // QUAD):
            nc.scalar.dma_start(
                key_scale_pool[QUAD * quad : QUAD * quad + 4, :].bitcast(I32),
                keys_scales[0, 4 * quad : 4 * quad + 4, :].bitcast(I32),
            )
        key_word_pool = keep.tile([P, T], U16, name="key_word_pool")
        nc.sync.dma_start(key_word_pool[:].bitcast(I32), keys_words[0].bitcast(I32))
        q_raw = {}
        for name, src in (("a", query), ("b", query2), ("ta", dquery)):
            q_raw[name] = keep.tile([P, PACK, Q], F32, name="q_raw_" + name, tag="q_raw_" + name, align_bytes=MX_ALIGN)
            nc.sync.dma_start(q_raw[name][:], src.rearrange("(p t) q -> p t q", t=PACK))
        val_halves = []
        for half in range(2):
            half_tile = keep.tile([P, T // 2], F32, name="val_half_%d" % half, tag="val_half_%d" % half)
            nc.sync.dma_start(half_tile[:], vals[0:P, half * T // 2 : (half + 1) * T // 2])
            val_halves.append(half_tile)
        os_col = keep.tile([P, PACK], F32, name="os_col")
        nc.sync.dma_start(os_col[:], slot_factor[0].rearrange("(p t) -> p t", t=PACK))
        val_pool = {}
        for blk in range(1, E_BLOCKS):
            if blk == E_BLOCKS - 1:
                val_pool[blk] = tail.tile([P, T], F32, name="val_pool_last", align_bytes=MX_ALIGN, offset=0)
            else:
                val_pool[blk] = keep.tile([P, T], F32, name="val_pool_%d" % blk)
            nc.sync.dma_start(val_pool[blk][:], vals[blk * P : (blk + 1) * P, :])

        ident = keep.tile([P, P], F32, name="ident")
        make_identity(nc, ident[:])

        q_codes, q_scales = {}, {}

        def quantize_query(name):
            grouped = keep.tile([P, Q * PACK], BF16, name="q_grouped_" + name, align_bytes=MX_ALIGN)
            nc.scalar.activation(
                grouped[:].rearrange("p (c i t) -> p c t i", i=LINE, t=PACK),
                q_raw[name][:].rearrange("p t (c i) -> p c t i", i=LINE),
                ACT.Copy,
            )
            q_codes[name] = keep.tile([P, Q], U32, name="q_codes_" + name, align_bytes=MX_ALIGN)
            q_scales[name] = keep.tile([P, Q], U8, name="q_scales_" + name, align_bytes=MX_ALIGN)
            nc.vector.quantize_mx(out=q_codes[name][:].bitcast(FP8X4), scales=q_scales[name][:], in_=grouped[:])

        key_words = keep.tile([P, I], U16, name="key_words", align_bytes=MX_ALIGN)
        nc.vector.tensor_copy(key_words[:], key_word_pool[:].indirect(offsets[:]))
        quantize_query("a")
        key_scales = keep.tile([P, I], U8, name="key_scales", tag="q_raw_a", align_bytes=MX_ALIGN)
        half_cols = I // GROUP // 2
        for half in range(2):
            nc.vector.tensor_copy(
                key_scales[:, half * I // 2 : (half + 1) * I // 2],
                key_scale_pool[:].indirect(offsets[:, half * half_cols : (half + 1) * half_cols]),
            )
        quantize_query("b")
        quantize_query("ta")

        score = {}
        for name, width in (("a", I // 2), ("b", I), ("ta", I)):
            score[name] = psum.tile([P, I], F32, name="score_" + name, tag="bank_" + name)
            for lo in range(0, I, width):
                nc.tensor.matmul_mx(
                    out=score[name][:, lo : lo + width],
                    lhsT=q_codes[name][:].bitcast(FP8X4),
                    lhsT_scale=q_scales[name][:],
                    rhs=key_words[:, lo : lo + width].bitcast(FP4X4),
                    rhs_scale=key_scales[:, lo : lo + width],
                    start=True,
                    stop=True,
                )

        neg_max_a = keep.tile([P, 1], F32, name="neg_max_a")
        nc.vector.tensor_reduce(neg_max_a[:], score["a"][:], AX.X, ALU.max, negate=True)
        page_max_b = keep.tile([P, G], F32, name="page_max_b")
        nc.vector.tensor_reduce(page_max_b[:], score["b"][:].rearrange("p (g j) -> p g j", j=PAGE), AX.X, ALU.max)

        val_bf16 = keep.tile([P, T], BF16, name="val_bf16", tag="val_bf16")
        nc.scalar.activation(val_bf16[:, 0 : T // 2], val_halves[0][:], ACT.Copy)
        pa_tpa = keep.tile([P, 2 * I], F32, name="pa_tpa", tag="val_half_0")
        pa, tpa = pa_tpa[:, 0:I], pa_tpa[:, I : 2 * I]
        z = keep.tile([P, 1], F32, name="z")
        nc.scalar.activation(pa, score["a"][:], ACT.Exp, bias=neg_max_a[:], accum_out=z[:])
        b_shifted = keep.tile([P, I], F32, name="b_shifted")
        nc.vector.tensor_tensor(
            b_shifted[:].rearrange("p (g j) -> p g j", j=PAGE),
            score["b"][:].rearrange("p (g j) -> p g j", j=PAGE),
            page_max_b[:].unsqueeze(2).broadcast_to([P, G, PAGE]),
            ALU.subtract,
        )
        tz = keep.tile([P, 1], F32, name="tz")
        nc.vector.scalar_tensor_tensor(tpa, score["ta"][:], 1.0, pa, ALU.mult, ALU.mult, accum_out=tz[:])
        nc.scalar.activation(val_bf16[:, T // 2 : T], val_halves[1][:], ACT.Copy)
        pb = keep.tile([P, PACK, P], F32, name="pb", tag="val_half_1")
        nc.scalar.activation(
            pb[:].rearrange("p t s -> p s t"), b_shifted[:].rearrange("p (s t) -> p s t", t=PACK), ACT.Exp
        )
        picked_0 = keep.tile([P, I], BF16, name="v_picked_0")
        nc.scalar.activation(picked_0[:], val_bf16[:].indirect(offsets[:]), ACT.Copy)

        rz = keep.tile([P, 1], F32, name="rz")
        nc.vector.reciprocal(rz[:], z[:])
        neg_mean = keep.tile([P, 1], F32, name="neg_mean")
        nc.gpsimd.tensor_scalar(neg_mean[:], tz[:], rz[:], -1.0, ALU.mult, ALU.mult)
        neg_mean_rz = keep.tile([P, 1], F32, name="neg_mean_rz")
        nc.gpsimd.tensor_scalar(neg_mean_rz[:], neg_mean[:], rz[:], 1.0, ALU.mult, ALU.mult)

        sums_t = psum.tile([P, Q], F32, name="sums_t")
        for j in range(PAGE):
            nc.tensor.matmul(
                sums_t[:], pa_tpa[:, j : 2 * I : PAGE], ident[:], start=(j == 0), stop=(j == PAGE - 1), is_transpose=True
            )
        pb_t = psum.tile([P, PACK, Q], F32, name="pb_t", tag="bank_pb")
        for t in range(PACK):
            nc.tensor.transpose(pb_t[:, t, :], pb[:, t, :], ident[:])

        sums_sb = keep.tile([P, Q], F32, name="sums_sb", tag="val_bf16")
        nc.scalar.copy(sums_sb[:], sums_t[:])
        sa_tsa = psum.tile([P, 2 * G], F32, name="sa_tsa", tag="bank_a")
        nc.tensor.transpose(sa_tsa[:], sums_sb[:], ident[:])
        share_parts = keep.tile([P, 2, G], F32, name="share_parts")
        nc.scalar.activation(share_parts[:, 0, :], sa_tsa[:, 0:G], ACT.Copy, scale=neg_mean_rz[:])
        nc.scalar.activation(share_parts[:, 1, :], sa_tsa[:, G : 2 * G], ACT.Copy, scale=rz[:])
        t_share = keep.tile([P, G], F32, name="t_share")
        nc.gpsimd.tensor_tensor(t_share[:], share_parts[:, 0, :], share_parts[:, 1, :], ALU.add)

        pbo_t = keep.tile([P, PACK, Q], F32, name="pbo_t")
        for t in range(PACK):
            nc.scalar.activation(pbo_t[:, t, :], pb_t[:, t, :], ACT.Copy, scale=os_col[:, t : t + 1])

        def pick_on_vector(blk):
            picked = keep.tile([P, I], BF16, name="v_picked_%d" % blk)
            nc.vector.tensor_copy(picked[:], val_pool[blk][:].indirect(offsets[:]))
            return picked

        def turn_values(name, picked_blocks, bank):
            n = len(picked_blocks)
            turned = psum.tile([P, n, 2, P], F32, name="v_turned_" + name, tag=bank)
            for b, picked in enumerate(picked_blocks):
                pairs = picked[:].bitcast(F32)
                for u in range(2):
                    nc.tensor.transpose(turned[:, b, u, :], pairs[:, u : I // 2 : 2], ident[:])
            grouped = keep.tile([P, n * P * PACK], BF16, name="v_grouped_" + name, align_bytes=MX_ALIGN)
            nc.scalar.copy(
                grouped[:].bitcast(F32).rearrange("p (b e u) -> p b e u", b=n, u=2),
                turned[:].rearrange("p b u e -> p b e u"),
            )
            return grouped

        grouped_01 = turn_values("01", [picked_0, pick_on_vector(1)], "bank_a")

        sb = keep.tile([P, G], F32, name="sb")
        nc.vector.tensor_reduce(sb[:], pb[:].rearrange("p t (g h) -> p g t h", h=2), AX.XY, ALU.add)
        rsb = keep.tile([P, G], F32, name="rsb")
        nc.vector.reciprocal(rsb[:], sb[:])
        tr = keep.tile([P, P], F32, name="tr")
        nc.gpsimd.tensor_tensor(
            tr[:].rearrange("p (g h) -> p g h", h=2),
            t_share[:].unsqueeze(2).broadcast_to([P, G, 2]),
            rsb[:].unsqueeze(2).broadcast_to([P, G, 2]),
            ALU.mult,
        )
        tr_t = psum.tile([P, Q], F32, name="tr_t", tag="bank_b")
        nc.tensor.transpose(tr_t[:], tr[:], ident[:])

        grouped_2 = turn_values("2", [pick_on_vector(2)], "bank_pb")
        grouped_3 = turn_values("3", [pick_on_vector(3)], "bank_v3")

        w_grouped = tail.tile([P, Q * PACK], BF16, name="w_grouped", align_bytes=MX_ALIGN, offset=0)
        v_codes = tail.tile([P, E], U32, name="v_codes", align_bytes=MX_ALIGN, offset=2 * Q * PACK)
        v_scales = keep.tile([P, E], U8, name="v_scales", align_bytes=MX_ALIGN)
        w_codes = keep.tile([P, Q], U32, name="w_codes", align_bytes=MX_ALIGN)
        w_scales = keep.tile([P, Q], U8, name="w_scales", align_bytes=MX_ALIGN)

        def quantize_values(lo, hi, grouped):
            nc.vector.quantize_mx(out=v_codes[:, lo:hi].bitcast(FP8X4), scales=v_scales[:, lo:hi], in_=grouped[:])

        nc.vector.tensor_tensor(
            w_grouped[:].rearrange("p (c i t) -> p c t i", i=LINE, t=PACK),
            tr_t[:].rearrange("p (c i) -> p c i", i=LINE).unsqueeze(2).broadcast_to([P, Q // LINE, PACK, LINE]),
            pbo_t[:].rearrange("p t (c i) -> p c t i", i=LINE),
            ALU.mult,
        )
        quantize_values(0, 2 * P, grouped_01)
        nc.vector.quantize_mx(out=w_codes[:].bitcast(FP8X4), scales=w_scales[:], in_=w_grouped[:])
        quantize_values(2 * P, 3 * P, grouped_2)
        quantize_values(3 * P, E, grouped_3)

        for lo, hi, bank in ((0, 2 * P, "bank_ta"), (2 * P, 3 * P, "bank_out"), (3 * P, E, "bank_b")):
            acc = psum.tile([Q, hi - lo], F32, name="acc_%d" % lo, tag=bank)
            nc.tensor.matmul_mx(
                out=acc[:],
                lhsT=w_codes[:].bitcast(FP8X4),
                lhsT_scale=w_scales[:],
                rhs=v_codes[:, lo:hi].bitcast(FP8X4),
                rhs_scale=v_scales[:, lo:hi],
                start=True,
                stop=True,
            )
            result = keep.tile([Q, hi - lo], F32, name="result_%d" % lo)
            if hi < E:
                nc.scalar.copy(result[:], acc[:])
            else:
                nc.vector.tensor_copy(result[:], acc[:])
            if lo == 2 * P:
                nc.scalar.dma_start(out[:, lo:hi], result[:])
            else:
                nc.sync.dma_start(out[:, lo:hi], result[:])
